import numpy as np
import ml_dtypes


def mxq(x, axis, fmt="e4m3"):
    dtype, down = {"e4m3": (ml_dtypes.float8_e4m3fn, 7), "e5m2": (ml_dtypes.float8_e5m2, 14)}[fmt]
    v = np.moveaxis(np.asarray(x, np.float32).astype(ml_dtypes.bfloat16).astype(np.float64), axis, -1)
    blocks = v.reshape(v.shape[:-1] + (-1, 32))
    amax = np.abs(blocks).max(-1, keepdims=True)
    byte = np.maximum(np.where(amax > 0, np.frexp(amax)[1] - 1 + 127, 0) - down, 1)
    scale = np.exp2(byte - 127.0)
    codes = (blocks / scale).astype(np.float32).astype(dtype).astype(np.float64)
    return np.moveaxis((codes * scale).reshape(v.shape), -1, axis)


WIDE = False


def mx_kscale(k):
    if not WIDE:
        return np.ones(k)
    levels = np.array([10, -10, 5, -5, 0])
    if k % 512:
        return np.exp2(np.random.permutation(np.resize(levels, k // 32))).repeat(32)
    a = np.empty((k // 512, 16))
    for p in range(k // 512):
        a[p, :8] = np.random.permutation(np.resize(levels, 8))
        for g in range(8):
            far = levels[np.abs(levels - a[p, g]) >= 10]
            a[p, g + 8] = far[np.random.randint(len(far))]
    return np.exp2(a.ravel()).repeat(32)


def f64(x):
    return np.asarray(x).astype(np.float64)


def striped(idx):
    return np.tile(idx.reshape(-1, 16).T, (8, 1)).astype(np.uint16)


def unstriped(offs):
    return offs[:16].T.reshape(-1).astype(np.int64)


def striped8(idx):
    return np.concatenate([x.reshape(-1, 16).T for x in idx]).astype(np.uint16)


def runs(offs, k):
    lists = np.stack([offs[16 * r : 16 * r + 16].T.reshape(-1) for r in range(8)]).astype(np.int64)
    return lists[np.arange(k) % 512 // 64]


def pack_weight(w):
    k, n = w.shape
    w = f64(np.asarray(w, np.float32).astype(ml_dtypes.bfloat16)).reshape(k // 32, 32, n)
    amax = np.abs(w).max(1)
    byte = np.clip(np.where(amax > 0, np.frexp(amax)[1] - 1 + 127 - 7, 1), 1, 254)
    scaled = (w * np.exp2(127.0 - byte)[:, None, :]).reshape(k, n).astype(np.float32)
    words = np.ascontiguousarray(scaled.reshape(k // 512, 128, 4, n).transpose(0, 1, 3, 2)).astype(ml_dtypes.float8_e4m3fn).view(np.uint8)
    return words, np.ascontiguousarray(byte.astype(np.uint8).reshape(k // 512, 16, n))


def unpack_weight(words, scales):
    g, p, n, _ = words.shape
    vals = np.ascontiguousarray(words).view(ml_dtypes.float8_e4m3fn).astype(np.float64) * np.repeat(np.exp2(scales.astype(np.float64) - 127.0), 8, axis=1)[..., None]
    return vals.transpose(0, 1, 3, 2).reshape(g * 512, n)


K, T, S, N, H = 512, 2048, 512, 512, 512


def setup_inputs():
    n = np.random.standard_normal
    s = mx_kscale(K)[:, None]
    u = mx_kscale(H)
    packed_xT = pack_weight(n((K, T)) * s)
    return {
        "x_words": packed_xT[0],
        "x_scales": packed_xT[1],
        "w1": (n((K, H)) / np.sqrt(K) / s).astype(np.float32),
        "gn": (np.random.uniform(0.5, 1.5, (H, 1)) * u[:, None]).astype(np.float32),
        "w2": (n((H, N)) / np.sqrt(H) / u[:, None]).astype(np.float32),
        "offs": striped(np.random.permutation(T)[:S]),
        "n1": striped8(np.stack([np.random.permutation(S) for _ in range(8)])),
        "n2": striped8(np.stack([np.random.permutation(S) for _ in range(8)])),
        "n3": striped8(np.stack([np.random.permutation(S) for _ in range(8)])),
        "n4": striped8(np.stack([np.random.permutation(S) for _ in range(8)])),
    }


def reference(x_words, x_scales, w1, gn, w2, offs, n1, n2, n3, n4):
    xq = unpack_weight(x_words, x_scales)[:, unstriped(offs)]
    y = mxq(f64(w1), 0, "e4m3").T @ xq
    z = f64(gn) * (y / (np.abs(y[np.arange(H)[:, None], runs(n1, H)]) + 0.5))
    h = mxq(f64(w2), 0, "e4m3").T @ mxq(z, 0, "e4m3")
    return y * (h[np.arange(N)[:, None], runs(n2, N)] - h) + 0.5 * ((y[np.arange(H)[:, None], runs(n4, H)]) * (h[np.arange(N)[:, None], runs(n3, N)] - h))

@@ -1,0 +1,187 @@
+from contextlib import ExitStack
+
+import concourse.mybir as mybir
+from concourse.masks import make_identity
+
+K, T, S, N, H = 512, 2048, 512, 512, 512
+FLOPS = 2 * K * H * S + 2 * H * N * S
+
+F32 = mybir.dt.float32
+BF16 = mybir.dt.bfloat16
+I32 = mybir.dt.int32
+U32 = mybir.dt.uint32
+U16 = mybir.dt.uint16
+U8 = mybir.dt.uint8
+FP8X4 = mybir.dt.float8_e4m3fn_x4
+ACT = mybir.ActivationFunctionType
+MULT = mybir.AluOpType.mult
+ADD = mybir.AluOpType.add
+SUBTRACT = mybir.AluOpType.subtract
+
+P = 128
+PACK = 4
+HALF = S // 2
+LIST_COLS = S // 16
+
+
+def deal_weight(nc, raw, grouped):
+    nc.vector.tensor_copy(
+        out=grouped[:].rearrange("p (t m j) -> p m j t", t=PACK, j=PACK),
+        in_=raw[:].rearrange("p j (m t) -> p m j t", t=PACK),
+    )
+
+
+def tile_picked_skipflowbnorm_none_p_kernel(tc, x_words, x_scales, w1, gn, w2, offs, n1, n2, n3, n4, out):
+    nc = tc.nc
+    tiles = range(PACK)
+    halves = [slice(0, HALF), slice(HALF, S)]
+    list_halves = [slice(0, LIST_COLS // 2), slice(LIST_COLS // 2, LIST_COLS)]
+    out_rows = out.rearrange("(p t) n -> t p n", t=PACK)
+
+    with ExitStack() as ctx:
+        keep = ctx.enter_context(tc.tile_pool(name="keep", bufs=1))
+        psum = ctx.enter_context(tc.psum_pool(name="psum", bufs=1))
+
+        def bank(b, name):
+            return psum.tile([P, S], F32, name=name, tag=f"bank{b}")
+
+        def load_list(src, name):
+            lst = keep.tile([P, LIST_COLS], U16, name=name)
+            nc.sync.dma_start(lst[:], src)
+            return lst
+
+        x_bytes = keep.tile([P, T], U8, align_bytes=64)
+        nc.vector.memset(x_bytes[:].bitcast(I32), 0)
+        w1_raw = keep.tile([P, PACK, H], F32)
+        nc.sync.dma_start(w1_raw[:], w1.rearrange("(p j) c -> p j c", j=PACK))
+        for q in range(4):
+            nc.sync.dma_start(x_bytes[32 * q : 32 * q + 4, :].bitcast(I32), x_scales[0, 4 * q : 4 * q + 4, :].bitcast(I32))
+        offs_sb = load_list(offs, "offs_sb")
+        x_packed = keep.tile([P, T], I32, align_bytes=64)
+        nc.sync.dma_start(x_packed[:], x_words[0].rearrange("p n t -> p (n t)").bitcast(I32))
+        n1_sb = load_list(n1, "n1_sb")
+        gain = keep.tile([P, PACK], F32)
+        nc.sync.dma_start(gain[:], gn.rearrange("(p t) o -> p (t o)", t=PACK))
+        w2_raw = keep.tile([P, PACK, N], F32)
+        nc.sync.dma_start(w2_raw[:], w2.rearrange("(p j) c -> p j c", j=PACK))
+        n4_sb = load_list(n4, "n4_sb")
+        n2_sb = load_list(n2, "n2_sb")
+        n3_sb = load_list(n3, "n3_sb")
+
+        half_const = keep.tile([P, 1], F32)
+        nc.gpsimd.memset(half_const[:], 0.5)
+        identity = keep.tile([P, P], F32)
+        make_identity(nc, identity[:])
+
+        w1_grouped = keep.tile([P, PACK * H], BF16, align_bytes=64)
+        deal_weight(nc, w1_raw, w1_grouped)
+        picked_bytes = keep.tile([P, S], U8, align_bytes=64)
+        nc.vector.tensor_copy(picked_bytes[:], x_bytes[:].indirect(offs_sb[:]))
+        w1_codes = keep.tile([P, H], U32, align_bytes=64)
+        w1_scales = keep.tile([P, H], U8, align_bytes=64)
+        nc.vector.quantize_mx(out=w1_codes[:].bitcast(FP8X4), scales=w1_scales[:], in_=w1_grouped[:])
+        picked_words = keep.tile([P, S], U32, align_bytes=64)
+        nc.vector.tensor_copy(picked_words[:], x_packed[:].bitcast(U32).indirect(offs_sb[:]))
+
+        y_bank = [bank(t, f"y_bank{t}") for t in tiles]
+        for t in tiles:
+            cols = slice(P * t, P * (t + 1))
+            nc.tensor.matmul_mx(
+                out=y_bank[t][:],
+                lhsT=w1_codes[:, cols].bitcast(FP8X4),
+                lhsT_scale=w1_scales[:, cols],
+                rhs=picked_words[:].bitcast(FP8X4),
+                rhs_scale=picked_bytes[:],
+                start=True,
+                stop=True,
+            )
+
+        y_window = [keep.tile([P, 2 * S], F32, name=f"y_window{t}") for t in tiles]
+        h_window = [keep.tile([P, 2 * S], F32, name=f"h_window{t}") for t in tiles]
+        log_window = [keep.tile([P, S], F32, name=f"log_window{t}") for t in tiles]
+        y = [y_window[t][:, 0:S] for t in tiles]
+        y_abs = [y_window[t][:, S : 2 * S] for t in tiles]
+        h = [h_window[t][:, 0:S] for t in tiles]
+        recip = [h_window[t][:, S : 2 * S] for t in tiles]
+
+        for t in tiles:
+            nc.scalar.activation(y_abs[t], y_bank[t][:], ACT.Abs)
+            nc.vector.tensor_copy(y[t], y_bank[t][:])
+            nc.scalar.activation(log_window[t][:], y_abs[t], ACT.Ln, bias=half_const[:])
+
+        w2_grouped = keep.tile([P, PACK * N], BF16, align_bytes=64)
+        deal_weight(nc, w2_raw, w2_grouped)
+        w2_codes = keep.tile([P, N], U32, align_bytes=64)
+        w2_scales = keep.tile([P, N], U8, align_bytes=64)
+        nc.vector.quantize_mx(out=w2_codes[:].bitcast(FP8X4), scales=w2_scales[:], in_=w2_grouped[:])
+
+        for c in range(2):
+            for t in tiles:
+                nc.scalar.activation(recip[t][:, halves[c]], log_window[t][:].indirect(n1_sb[:, list_halves[c]]), ACT.Exp, scale=-1.0)
+
+        for c in range(2):
+            z_rows = keep.tile([P, PACK, HALF], BF16, name=f"z_rows{c}", tag="z_then_sum")
+            for t in tiles:
+                nc.vector.scalar_tensor_tensor(z_rows[:, t, :], y_bank[t][:, halves[c]], gain[:, t : t + 1], recip[t][:, halves[c]], MULT, MULT)
+            z_grouped = keep.tile([P, PACK * HALF], BF16, name=f"z_grouped{c}", align_bytes=64)
+            nc.vector.tensor_copy(
+                out=z_grouped[:].rearrange("p (c i t) -> p c t i", i=4, t=PACK),
+                in_=z_rows[:].rearrange("p t (c i) -> p c t i", i=4),
+            )
+            z_codes = keep.tile([P, HALF], U32, name=f"z_codes{c}", align_bytes=64)
+            z_scales = keep.tile([P, HALF], U8, name=f"z_scales{c}", align_bytes=64)
+            nc.vector.quantize_mx(out=z_codes[:].bitcast(FP8X4), scales=z_scales[:], in_=z_grouped[:])
+            for pair in range(2):
+                h_bank = bank(4 + 2 * c + pair, f"h_bank{c}{pair}")
+                for u in range(2):
+                    t = 2 * pair + u
+                    cols = slice(P * t, P * (t + 1))
+                    nc.tensor.matmul_mx(
+                        out=h_bank[:, halves[u]],
+                        lhsT=w2_codes[:, cols].bitcast(FP8X4),
+                        lhsT_scale=w2_scales[:, cols],
+                        rhs=z_codes[:].bitcast(FP8X4),
+                        rhs_scale=z_scales[:],
+                        start=True,
+                        stop=True,
+                    )
+                    nc.scalar.copy(h[t][:, halves[c]], h_bank[:, halves[u]])
+
+        y_far = [keep.tile([P, S], F32, name=f"y_far{t}") for t in tiles]
+        for t in tiles:
+            nc.vector.tensor_scalar(y_far[t][:], y_window[t][:].indirect(n4_sb[:]), 0.5, 0.0, MULT, ADD)
+        minus_sum = keep.tile([P, PACK, S], F32, tag="z_then_sum")
+        for t in tiles:
+            nc.vector.scalar_tensor_tensor(minus_sum[:, t, :], y_far[t][:], -1.0, y[t], MULT, SUBTRACT)
+
+        last = PACK - 1
+        for t in tiles:
+            near = keep.tile([P, S], F32, name=f"near{t}")
+            far = keep.tile([P, S], F32, name=f"far{t}")
+            own = keep.tile([P, S], F32, name=f"own{t}")
+            result = keep.tile([P, S], F32, name=f"result{t}")
+            nc.vector.tensor_tensor(own[:], h[t], minus_sum[:, t, :], MULT)
+            nc.vector.tensor_tensor(near[:], h_window[t][:].indirect(n2_sb[:]), y[t], MULT)
+            if t < last:
+                nc.vector.tensor_tensor(far[:], h_window[t][:].indirect(n3_sb[:]), y_far[t][:], MULT)
+                turned_bank = bank(t % 2, f"turned_bank{t}")
+                for q in range(4):
+                    cols = slice(P * q, P * (q + 1))
+                    for i, term in enumerate((own, near, far)):
+                        nc.tensor.matmul(turned_bank[:, cols], term[:, cols], identity[:], start=(i == 0), stop=(i == 2), is_transpose=True)
+                turned = keep.tile([P, S], F32, name=f"turned{t}")
+                nc.scalar.copy(turned[:], turned_bank[:])
+                back_bank = bank(2 + t % 2, f"back_bank{t}")
+                for q in range(4):
+                    cols = slice(P * q, P * (q + 1))
+                    nc.tensor.transpose(back_bank[:, cols], turned[:, cols], identity[:])
+                nc.scalar.copy(result[:], back_bank[:])
+                nc.sync.dma_start(out_rows[t], result[:])
+            else:
+                partial = keep.tile([P, S], F32)
+                nc.vector.tensor_tensor(far[:, halves[0]], h_window[t][:].indirect(n3_sb[:, list_halves[0]]), y_far[t][:, halves[0]], MULT)
+                nc.vector.tensor_tensor(partial[:], own[:], near[:], ADD)
+                nc.vector.tensor_tensor(far[:, halves[1]], h_window[t][:].indirect(n3_sb[:, list_halves[1]]), y_far[t][:, halves[1]], MULT)
+                for c in range(2):
+                    nc.vector.tensor_tensor(result[:, halves[c]], partial[:, halves[c]], far[:, halves[c]], ADD)
+                    nc.sync.dma_start(out_rows[t][:, halves[c]], result[:, halves[c]])

@@ -26,8 +26,8 @@ LIST_COLS = S // 16
 
 def deal_weight(nc, raw, grouped):
     nc.vector.tensor_copy(
-        out=grouped[:].rearrange("p (t m j) -> p m j t", t=PACK, j=PACK),
-        in_=raw[:].rearrange("p j (m t) -> p m j t", t=PACK),
+        out=grouped[:].rearrange("p (t a r j) -> p t a j r", t=PACK, r=4, j=PACK),
+        in_=raw[:].rearrange("p j (a t r) -> p t a j r", t=PACK, r=4),
     )
 
 
@@ -36,7 +36,9 @@ def tile_picked_skipflowbnorm_none_p_kernel(tc, x_words, x_scales, w1, gn, w2, o
     tiles = range(PACK)
     halves = [slice(0, HALF), slice(HALF, S)]
     list_halves = [slice(0, LIST_COLS // 2), slice(LIST_COLS // 2, LIST_COLS)]
-    out_rows = out.rearrange("(p t) n -> t p n", t=PACK)
+    out_rows = out.rearrange("(a t r) n -> t a r n", t=PACK, r=4)
+    w2_rows = w2.rearrange("(a t r) n -> t a r n", t=PACK, r=4)
+    gn_rows = gn.rearrange("(a t r) o -> t a r o", t=PACK, r=4)
 
     with ExitStack() as ctx:
         keep = ctx.enter_context(tc.tile_pool(name="keep", bufs=1))
@@ -60,16 +62,24 @@ def tile_picked_skipflowbnorm_none_p_kernel(tc, x_words, x_scales, w1, gn, w2, o
         x_packed = keep.tile([P, T], I32, align_bytes=64)
         nc.sync.dma_start(x_packed[:], x_words[0].rearrange("p n t -> p (n t)").bitcast(I32))
         n1_sb = load_list(n1, "n1_sb")
-        gain = keep.tile([P, PACK], F32)
-        nc.sync.dma_start(gain[:], gn.rearrange("(p t) o -> p (t o)", t=PACK))
         w2_raw = keep.tile([P, PACK, N], F32)
-        nc.sync.dma_start(w2_raw[:], w2.rearrange("(p j) c -> p j c", j=PACK))
+        for t in tiles:
+            nc.sync.dma_start(w2_raw[:, t, :], w2_rows[t])
         n4_sb = load_list(n4, "n4_sb")
+        gain = [keep.tile([P, 1], F32, name=f"gain{t}") for t in tiles]
+        for t in tiles:
+            nc.sync.dma_start(gain[t][:], gn_rows[t])
         n2_sb = load_list(n2, "n2_sb")
         n3_sb = load_list(n3, "n3_sb")
 
         half_const = keep.tile([P, 1], F32)
         nc.gpsimd.memset(half_const[:], 0.5)
+        warm = keep.tile([P, 1], F32)
+        nc.scalar.activation(warm[:], half_const[:], ACT.Ln)
+        last = PACK - 1
+        y_window = [keep.tile([P, 2 * S], F32, name=f"y_window{t}") for t in range(last)]
+        for t in range(last):
+            nc.vector.memset(y_window[t][:, S : 2 * S], 0.0)
         identity = keep.tile([P, P], F32)
         make_identity(nc, identity[:])
 
@@ -80,34 +90,38 @@ def tile_picked_skipflowbnorm_none_p_kernel(tc, x_words, x_scales, w1, gn, w2, o
         w1_codes = keep.tile([P, H], U32, align_bytes=64)
         w1_scales = keep.tile([P, H], U8, align_bytes=64)
         nc.vector.quantize_mx(out=w1_codes[:].bitcast(FP8X4), scales=w1_scales[:], in_=w1_grouped[:])
-        picked_words = keep.tile([P, S], U32, align_bytes=64)
-        nc.vector.tensor_copy(picked_words[:], x_packed[:].bitcast(U32).indirect(offs_sb[:]))
+        y_bank = []
+        for c in range(2):
+            picked_words = keep.tile([P, HALF], U32, name=f"picked_words{c}", align_bytes=64)
+            nc.vector.tensor_copy(picked_words[:], x_packed[:].bitcast(U32).indirect(offs_sb[:, list_halves[c]]))
+            y_bank.append([bank(2 * c + pair, f"y_bank{c}{pair}") for pair in range(2)])
+            for t in tiles:
+                cols = slice(P * t, P * (t + 1))
+                nc.tensor.matmul_mx(
+                    out=y_bank[c][t // 2][:, halves[t % 2]],
+                    lhsT=w1_codes[:, cols].bitcast(FP8X4),
+                    lhsT_scale=w1_scales[:, cols],
+                    rhs=picked_words[:].bitcast(FP8X4),
+                    rhs_scale=picked_bytes[:, halves[c]],
+                    start=True,
+                    stop=True,
+                )
 
-        y_bank = [bank(t, f"y_bank{t}") for t in tiles]
-        for t in tiles:
-            cols = slice(P * t, P * (t + 1))
-            nc.tensor.matmul_mx(
-                out=y_bank[t][:],
-                lhsT=w1_codes[:, cols].bitcast(FP8X4),
-                lhsT_scale=w1_scales[:, cols],
-                rhs=picked_words[:].bitcast(FP8X4),
-                rhs_scale=picked_bytes[:],
-                start=True,
-                stop=True,
-            )
-
-        y_window = [keep.tile([P, 2 * S], F32, name=f"y_window{t}") for t in tiles]
         h_window = [keep.tile([P, 2 * S], F32, name=f"h_window{t}") for t in tiles]
-        log_window = [keep.tile([P, S], F32, name=f"log_window{t}") for t in tiles]
-        y = [y_window[t][:, 0:S] for t in tiles]
-        y_abs = [y_window[t][:, S : 2 * S] for t in tiles]
+        log_window = [keep.tile([P, S], F32, name=f"log_window{t}", tag=f"log_window{t}") for t in tiles]
+        y = [y_window[t][:, 0:S] for t in range(last)]
+        y_abs = keep.tile([P, PACK, S], F32)
         h = [h_window[t][:, 0:S] for t in tiles]
         recip = [h_window[t][:, S : 2 * S] for t in tiles]
 
-        for t in tiles:
-            nc.scalar.activation(y_abs[t], y_bank[t][:], ACT.Abs)
-            nc.vector.tensor_copy(y[t], y_bank[t][:])
-            nc.scalar.activation(log_window[t][:], y_abs[t], ACT.Ln, bias=half_const[:])
+        for c in range(2):
+            for pair in range(2):
+                nc.scalar.activation(y_abs[:, 2 * pair : 2 * pair + 2, halves[c]], y_bank[c][pair][:].rearrange("p (u n) -> p u n", u=2), ACT.Abs)
+                for t in (2 * pair, 2 * pair + 1):
+                    if t < last:
+                        nc.vector.tensor_copy(y[t][:, halves[c]], y_bank[c][pair][:, halves[t % 2]])
+                    if c == 1:
+                        nc.scalar.activation(log_window[t][:], y_abs[:, t, :], ACT.Ln, bias=half_const[:])
 
         w2_grouped = keep.tile([P, PACK * N], BF16, align_bytes=64)
         deal_weight(nc, w2_raw, w2_grouped)
@@ -118,12 +132,15 @@ def tile_picked_skipflowbnorm_none_p_kernel(tc, x_words, x_scales, w1, gn, w2, o
         for c in range(2):
             for t in tiles:
                 nc.scalar.activation(recip[t][:, halves[c]], log_window[t][:].indirect(n1_sb[:, list_halves[c]]), ACT.Exp, scale=-1.0)
+        y_last = keep.tile([P, S], F32, tag=f"log_window{last}")
+        y.append(y_last[:])
 
         for c in range(2):
-            z_rows = keep.tile([P, PACK, HALF], BF16, name=f"z_rows{c}", tag="z_then_sum")
+            z_rows = keep.tile([P, PACK, HALF], BF16, name=f"z_rows{c}", tag=f"z_rows{c}")
             for t in tiles:
-                nc.vector.scalar_tensor_tensor(z_rows[:, t, :], y_bank[t][:, halves[c]], gain[:, t : t + 1], recip[t][:, halves[c]], MULT, MULT)
-            z_grouped = keep.tile([P, PACK * HALF], BF16, name=f"z_grouped{c}", align_bytes=64)
+                nc.vector.scalar_tensor_tensor(z_rows[:, t, :], y_bank[c][t // 2][:, halves[t % 2]], gain[t][:], recip[t][:, halves[c]], MULT, MULT)
+            nc.scalar.copy(y_last[:, halves[c]], y_bank[c][last // 2][:, halves[last % 2]])
+            z_grouped = keep.tile([P, PACK * HALF], BF16, name=f"z_grouped{c}", tag=f"z_grouped{c}", align_bytes=64)
             nc.vector.tensor_copy(
                 out=z_grouped[:].rearrange("p (c i t) -> p c t i", i=4, t=PACK),
                 in_=z_rows[:].rearrange("p t (c i) -> p c t i", i=4),
@@ -132,7 +149,7 @@ def tile_picked_skipflowbnorm_none_p_kernel(tc, x_words, x_scales, w1, gn, w2, o
             z_scales = keep.tile([P, HALF], U8, name=f"z_scales{c}", align_bytes=64)
             nc.vector.quantize_mx(out=z_codes[:].bitcast(FP8X4), scales=z_scales[:], in_=z_grouped[:])
             for pair in range(2):
-                h_bank = bank(4 + 2 * c + pair, f"h_bank{c}{pair}")
+                h_bank = bank(2 * c + pair, f"h_bank{c}{pair}")
                 for u in range(2):
                     t = 2 * pair + u
                     cols = slice(P * t, P * (t + 1))
@@ -147,41 +164,52 @@ def tile_picked_skipflowbnorm_none_p_kernel(tc, x_words, x_scales, w1, gn, w2, o
                     )
                     nc.scalar.copy(h[t][:, halves[c]], h_bank[:, halves[u]])
 
-        y_far = [keep.tile([P, S], F32, name=f"y_far{t}") for t in tiles]
-        for t in tiles:
+        y_far = [keep.tile([P, S], F32, name=f"y_far{t}") for t in range(last)]
+        for t in range(last):
             nc.vector.tensor_scalar(y_far[t][:], y_window[t][:].indirect(n4_sb[:]), 0.5, 0.0, MULT, ADD)
-        minus_sum = keep.tile([P, PACK, S], F32, tag="z_then_sum")
-        for t in tiles:
-            nc.vector.scalar_tensor_tensor(minus_sum[:, t, :], y_far[t][:], -1.0, y[t], MULT, SUBTRACT)
+        y_far.append(keep.tile([P, S], F32, name="y_far_last", tag="z_grouped1", align_bytes=64))
+        for c in range(2):
+            nc.vector.tensor_scalar(y_far[last][:, halves[c]], y_last[:].indirect(n4_sb[:, list_halves[c]]), 0.5, 0.0, MULT, ADD)
 
-        last = PACK - 1
+        def add_turned(target, terms):
+            for i, term in enumerate(terms):
+                for q in range(4):
+                    cols = slice(P * q, P * (q + 1))
+                    first, final = (i == 0 and q == 0), (i == len(terms) - 1 and q == 3)
+                    nc.tensor.matmul(target[:, cols], term[:, cols], identity[:], start=first, stop=final, is_transpose=True)
+
+        sum_turned = keep.tile([P, PACK, S], F32, tag="z_rows1")
+        minus_sum = []
+        for t in tiles:
+            sum_bank = bank(4 + t, f"sum_bank{t}")
+            add_turned(sum_bank, (y[t], y_far[t]))
+            nc.scalar.activation(sum_turned[:, t, :], sum_bank[:], ACT.Copy, scale=-1.0)
+            minus_sum.append(bank(4 + t, f"minus_sum{t}"))
+            add_turned(minus_sum[t], (sum_turned[:, t, :],))
+
         for t in tiles:
             near = keep.tile([P, S], F32, name=f"near{t}")
             far = keep.tile([P, S], F32, name=f"far{t}")
             own = keep.tile([P, S], F32, name=f"own{t}")
             result = keep.tile([P, S], F32, name=f"result{t}")
-            nc.vector.tensor_tensor(own[:], h[t], minus_sum[:, t, :], MULT)
             nc.vector.tensor_tensor(near[:], h_window[t][:].indirect(n2_sb[:]), y[t], MULT)
             if t < last:
                 nc.vector.tensor_tensor(far[:], h_window[t][:].indirect(n3_sb[:]), y_far[t][:], MULT)
+                nc.vector.tensor_tensor(own[:], h[t], minus_sum[t][:], MULT)
                 turned_bank = bank(t % 2, f"turned_bank{t}")
-                for q in range(4):
-                    cols = slice(P * q, P * (q + 1))
-                    for i, term in enumerate((own, near, far)):
-                        nc.tensor.matmul(turned_bank[:, cols], term[:, cols], identity[:], start=(i == 0), stop=(i == 2), is_transpose=True)
+                add_turned(turned_bank, (near, far, own))
                 turned = keep.tile([P, S], F32, name=f"turned{t}")
                 nc.scalar.copy(turned[:], turned_bank[:])
                 back_bank = bank(2 + t % 2, f"back_bank{t}")
-                for q in range(4):
-                    cols = slice(P * q, P * (q + 1))
-                    nc.tensor.transpose(back_bank[:, cols], turned[:, cols], identity[:])
+                add_turned(back_bank, (turned,))
                 nc.scalar.copy(result[:], back_bank[:])
                 nc.sync.dma_start(out_rows[t], result[:])
             else:
                 partial = keep.tile([P, S], F32)
+                nc.vector.tensor_tensor(own[:], h[t], minus_sum[t][:], MULT)
                 nc.vector.tensor_tensor(far[:, halves[0]], h_window[t][:].indirect(n3_sb[:, list_halves[0]]), y_far[t][:, halves[0]], MULT)
                 nc.vector.tensor_tensor(partial[:], own[:], near[:], ADD)
                 nc.vector.tensor_tensor(far[:, halves[1]], h_window[t][:].indirect(n3_sb[:, list_halves[1]]), y_far[t][:, halves[1]], MULT)
                 for c in range(2):
                     nc.vector.tensor_tensor(result[:, halves[c]], partial[:, halves[c]], far[:, halves[c]], ADD)
-                    nc.sync.dma_start(out_rows[t][:, halves[c]], result[:, halves[c]])
+                    nc.sync.dma_start(out_rows[t][:, :, halves[c]], result[:, halves[c]])

@@ -15,13 +15,16 @@ U8 = mybir.dt.uint8
 FP8X4 = mybir.dt.float8_e4m3fn_x4
 ACT = mybir.ActivationFunctionType
 MULT = mybir.AluOpType.mult
+MAX = mybir.AluOpType.max
 ADD = mybir.AluOpType.add
 SUBTRACT = mybir.AluOpType.subtract
 
 P = 128
 PACK = 4
 HALF = S // 2
+PIECES = [(0, 256, (0, 1)), (256, 128, (2,)), (384, 128, (3,))]
 LIST_COLS = S // 16
+TAIL = [(0, 384), (384, 128)]
 
 
 def deal_weight(nc, raw, grouped):
@@ -53,12 +56,12 @@ def tile_picked_skipflowbnorm_none_p_kernel(tc, x_words, x_scales, w1, gn, w2, o
             return lst
 
         x_bytes = keep.tile([P, T], U8, align_bytes=64)
-        nc.vector.memset(x_bytes[:].bitcast(I32), 0)
-        w1_raw = keep.tile([P, PACK, H], F32)
-        nc.sync.dma_start(w1_raw[:], w1.rearrange("(p j) c -> p j c", j=PACK))
+        nc.gpsimd.memset(x_bytes[:].bitcast(I32), 0)
+        offs_sb = load_list(offs, "offs_sb")
         for q in range(4):
             nc.sync.dma_start(x_bytes[32 * q : 32 * q + 4, :].bitcast(I32), x_scales[0, 4 * q : 4 * q + 4, :].bitcast(I32))
-        offs_sb = load_list(offs, "offs_sb")
+        w1_raw = keep.tile([P, PACK, H], F32)
+        nc.sync.dma_start(w1_raw[:], w1.rearrange("(p j) c -> p j c", j=PACK))
         x_packed = keep.tile([P, T], I32, align_bytes=64)
         nc.sync.dma_start(x_packed[:], x_words[0].rearrange("p n t -> p (n t)").bitcast(I32))
         n1_sb = load_list(n1, "n1_sb")
@@ -77,84 +80,103 @@ def tile_picked_skipflowbnorm_none_p_kernel(tc, x_words, x_scales, w1, gn, w2, o
         warm = keep.tile([P, 1], F32)
         nc.scalar.activation(warm[:], half_const[:], ACT.Ln)
         last = PACK - 1
-        y_window = [keep.tile([P, 2 * S], F32, name=f"y_window{t}") for t in range(last)]
-        for t in range(last):
+        y_window = [keep.tile([P, 2 * S], F32, name=f"y_window{t}") for t in tiles]
+        h_window = [keep.tile([P, 2 * S], F32, name=f"h_window{t}") for t in tiles]
+        for t in tiles:
             nc.vector.memset(y_window[t][:, S : 2 * S], 0.0)
+            nc.gpsimd.memset(h_window[t][:, S : 2 * S], 0.0)
         identity = keep.tile([P, P], F32)
         make_identity(nc, identity[:])
 
-        w1_grouped = keep.tile([P, PACK * H], BF16, align_bytes=64)
-        deal_weight(nc, w1_raw, w1_grouped)
         picked_bytes = keep.tile([P, S], U8, align_bytes=64)
         nc.vector.tensor_copy(picked_bytes[:], x_bytes[:].indirect(offs_sb[:]))
-        w1_codes = keep.tile([P, H], U32, align_bytes=64)
-        w1_scales = keep.tile([P, H], U8, align_bytes=64)
-        nc.vector.quantize_mx(out=w1_codes[:].bitcast(FP8X4), scales=w1_scales[:], in_=w1_grouped[:])
-        y_bank = []
-        for c in range(2):
-            picked_words = keep.tile([P, HALF], U32, name=f"picked_words{c}", align_bytes=64)
-            nc.vector.tensor_copy(picked_words[:], x_packed[:].bitcast(U32).indirect(offs_sb[:, list_halves[c]]))
-            y_bank.append([bank(2 * c + pair, f"y_bank{c}{pair}") for pair in range(2)])
-            for t in tiles:
-                cols = slice(P * t, P * (t + 1))
-                nc.tensor.matmul_mx(
-                    out=y_bank[c][t // 2][:, halves[t % 2]],
-                    lhsT=w1_codes[:, cols].bitcast(FP8X4),
-                    lhsT_scale=w1_scales[:, cols],
-                    rhs=picked_words[:].bitcast(FP8X4),
-                    rhs_scale=picked_bytes[:, halves[c]],
-                    start=True,
-                    stop=True,
-                )
+        w1_codes, w1_scales = [], []
+        w1_dealt = w1_raw[:].rearrange("p j (a t r) -> p t a j r", t=PACK, r=4)
+        for pair, copy in enumerate((nc.vector.tensor_copy, nc.scalar.copy)):
+            grouped = keep.tile([P, 2 * PACK * P], BF16, name=f"w1_grouped{pair}", align_bytes=64)
+            copy(grouped[:].rearrange("p (t a r j) -> p t a j r", t=2, r=4, j=PACK), w1_dealt[:, 2 * pair : 2 * pair + 2])
+            w1_codes.append(keep.tile([P, 2 * P], U32, name=f"w1_codes{pair}", align_bytes=64))
+            w1_scales.append(keep.tile([P, 2 * P], U8, name=f"w1_scales{pair}", align_bytes=64))
+            nc.vector.quantize_mx(out=w1_codes[pair][:].bitcast(FP8X4), scales=w1_scales[pair][:], in_=grouped[:])
 
-        h_window = [keep.tile([P, 2 * S], F32, name=f"h_window{t}") for t in tiles]
-        log_window = [keep.tile([P, S], F32, name=f"log_window{t}", tag=f"log_window{t}") for t in tiles]
-        y = [y_window[t][:, 0:S] for t in range(last)]
-        y_abs = keep.tile([P, PACK, S], F32)
+        picked_words = []
+        for c in range(2):
+            picked_words.append(keep.tile([P, HALF], U32, name=f"picked_words{c}", align_bytes=64))
+            nc.vector.tensor_copy(picked_words[c][:], x_packed[:].bitcast(U32).indirect(offs_sb[:, list_halves[c]]))
+
+        log_window = [keep.tile([P, S], F32, name=f"log_window{t}") for t in tiles]
+        y = [y_window[t][:, 0:S] for t in tiles]
         h = [h_window[t][:, 0:S] for t in tiles]
-        recip = [h_window[t][:, S : 2 * S] for t in tiles]
-
-        for c in range(2):
-            for pair in range(2):
-                nc.scalar.activation(y_abs[:, 2 * pair : 2 * pair + 2, halves[c]], y_bank[c][pair][:].rearrange("p (u n) -> p u n", u=2), ACT.Abs)
-                for t in (2 * pair, 2 * pair + 1):
-                    if t < last:
-                        nc.vector.tensor_copy(y[t][:, halves[c]], y_bank[c][pair][:, halves[t % 2]])
-                    if c == 1:
-                        nc.scalar.activation(log_window[t][:], y_abs[:, t, :], ACT.Ln, bias=half_const[:])
+        y_abs = keep.tile([P, PACK, S], F32, tag="recip")
+        for pair in range(2):
+            pair_tiles = (2 * pair, 2 * pair + 1)
+            for c in range(2):
+                y_bank = bank(2 * pair + c, f"y_bank{pair}{c}")
+                for u in range(2):
+                    cols = slice(P * u, P * (u + 1))
+                    nc.tensor.matmul_mx(
+                        out=y_bank[:, halves[u]],
+                        lhsT=w1_codes[pair][:, cols].bitcast(FP8X4),
+                        lhsT_scale=w1_scales[pair][:, cols],
+                        rhs=picked_words[c][:].bitcast(FP8X4),
+                        rhs_scale=picked_bytes[:, halves[c]],
+                        start=True,
+                        stop=True,
+                    )
+                abs_on_vector = (pair, c) == (1, 0)
+                if not abs_on_vector:
+                    nc.scalar.activation(y_abs[:, 2 * pair : 2 * pair + 2, halves[c]], y_bank[:].rearrange("p (u n) -> p u n", u=2), ACT.Abs)
+                for u, t in enumerate(pair_tiles):
+                    nc.vector.tensor_copy(y[t][:, halves[c]], y_bank[:, halves[u]])
+                if abs_on_vector:
+                    for u, t in enumerate(pair_tiles):
+                        nc.vector.scalar_tensor_tensor(y_abs[:, t, halves[c]], y_bank[:, halves[u]], -1.0, y[t][:, halves[c]], MULT, MAX)
+            for t in pair_tiles:
+                nc.scalar.activation(log_window[t][:], y_abs[:, t, :], ACT.Ln, bias=half_const[:])
 
         w2_grouped = keep.tile([P, PACK * N], BF16, align_bytes=64)
-        deal_weight(nc, w2_raw, w2_grouped)
+        w2_dealt = w2_raw[:].rearrange("p j (a t r) -> p t a r j", t=PACK, r=4)
+        for t in tiles:
+            target = w2_grouped[:, PACK * P * t : PACK * P * (t + 1)].rearrange("p (a r j) -> p a r j", r=4, j=PACK)
+            nc.gpsimd.tensor_scalar(target, w2_dealt[:, t], 1.0, 0.0, MULT, ADD)
         w2_codes = keep.tile([P, N], U32, align_bytes=64)
         w2_scales = keep.tile([P, N], U8, align_bytes=64)
         nc.vector.quantize_mx(out=w2_codes[:].bitcast(FP8X4), scales=w2_scales[:], in_=w2_grouped[:])
 
-        for c in range(2):
-            for t in tiles:
-                nc.scalar.activation(recip[t][:, halves[c]], log_window[t][:].indirect(n1_sb[:, list_halves[c]]), ACT.Exp, scale=-1.0)
-        y_last = keep.tile([P, S], F32, tag=f"log_window{last}")
-        y.append(y_last[:])
+        y_gain = keep.tile([P, PACK, S], F32)
+        for t in tiles:
+            nc.gpsimd.tensor_scalar(y_gain[:, t, :], y[t], gain[t][:], 0.0, MULT, ADD)
 
+        pieces = PIECES
+        recip = keep.tile([P, PACK, S], F32, tag="recip")
+        recip_last = keep.tile([P, S], F32)
+        nc.scalar.activation(recip_last[:], log_window[last][:], ACT.Exp, scale=-1.0)
         for c in range(2):
-            z_rows = keep.tile([P, PACK, HALF], BF16, name=f"z_rows{c}", tag=f"z_rows{c}")
-            for t in tiles:
-                nc.vector.scalar_tensor_tensor(z_rows[:, t, :], y_bank[c][t // 2][:, halves[t % 2]], gain[t][:], recip[t][:, halves[c]], MULT, MULT)
-            nc.scalar.copy(y_last[:, halves[c]], y_bank[c][last // 2][:, halves[last % 2]])
-            z_grouped = keep.tile([P, PACK * HALF], BF16, name=f"z_grouped{c}", tag=f"z_grouped{c}", align_bytes=64)
-            nc.vector.tensor_copy(
-                out=z_grouped[:].rearrange("p (c i t) -> p c t i", i=4, t=PACK),
-                in_=z_rows[:].rearrange("p t (c i) -> p c t i", i=4),
+            nc.vector.tensor_copy(recip[:, last, halves[c]], recip_last[:].indirect(n1_sb[:, list_halves[c]]))
+        for first, width, banks in pieces:
+            for t in range(last):
+                entries = n1_sb[:, first // 16 : (first + width) // 16]
+                nc.scalar.activation(recip[:, t, first : first + width], log_window[t][:].indirect(entries), ACT.Exp, scale=-1.0)
+
+        for g, (first, width, banks) in enumerate(pieces):
+            z_grouped = keep.tile([P, PACK * width], BF16, name=f"z_grouped{g}", tag=f"z_grouped{g}", align_bytes=64)
+            nc.vector.tensor_tensor(
+                z_grouped[:].rearrange("p (c i t) -> p c t i", i=4, t=PACK),
+                y_gain[:, :, first : first + width].rearrange("p t (c i) -> p c t i", i=4),
+                recip[:, :, first : first + width].rearrange("p t (c i) -> p c t i", i=4),
+                MULT,
             )
-            z_codes = keep.tile([P, HALF], U32, name=f"z_codes{c}", align_bytes=64)
-            z_scales = keep.tile([P, HALF], U8, name=f"z_scales{c}", align_bytes=64)
+            z_codes = keep.tile([P, width], U32, name=f"z_codes{g}", align_bytes=64)
+            z_scales = keep.tile([P, width], U8, name=f"z_scales{g}", align_bytes=64)
             nc.vector.quantize_mx(out=z_codes[:].bitcast(FP8X4), scales=z_scales[:], in_=z_grouped[:])
-            for pair in range(2):
-                h_bank = bank(2 * c + pair, f"h_bank{c}{pair}")
-                for u in range(2):
-                    t = 2 * pair + u
+            per_bank = S // width
+            for b, number in enumerate(banks):
+                h_bank = bank(number, f"h_bank{g}{b}")
+                for u in range(per_bank):
+                    t = per_bank * b + u
                     cols = slice(P * t, P * (t + 1))
                     nc.tensor.matmul_mx(
-                        out=h_bank[:, halves[u]],
+                        out=h_bank[:, width * u : width * (u + 1)],
                         lhsT=w2_codes[:, cols].bitcast(FP8X4),
                         lhsT_scale=w2_scales[:, cols],
                         rhs=z_codes[:].bitcast(FP8X4),
@@ -162,14 +184,14 @@ def tile_picked_skipflowbnorm_none_p_kernel(tc, x_words, x_scales, w1, gn, w2, o
                         start=True,
                         stop=True,
                     )
-                    nc.scalar.copy(h[t][:, halves[c]], h_bank[:, halves[u]])
+                for u in range(per_bank):
+                    t = per_bank * b + u
+                    nc.scalar.copy(h[t][:, first : first + width], h_bank[:, width * u : width * (u + 1)])
 
         y_far = [keep.tile([P, S], F32, name=f"y_far{t}") for t in range(last)]
-        for t in range(last):
+        y_far.append(keep.tile([P, S], F32, name="y_far_last", tag=f"z_grouped{len(pieces) - 1}", align_bytes=64))
+        for t in tiles:
             nc.vector.tensor_scalar(y_far[t][:], y_window[t][:].indirect(n4_sb[:]), 0.5, 0.0, MULT, ADD)
-        y_far.append(keep.tile([P, S], F32, name="y_far_last", tag="z_grouped1", align_bytes=64))
-        for c in range(2):
-            nc.vector.tensor_scalar(y_far[last][:, halves[c]], y_last[:].indirect(n4_sb[:, list_halves[c]]), 0.5, 0.0, MULT, ADD)
 
         def add_turned(target, terms):
             for i, term in enumerate(terms):
@@ -178,7 +200,7 @@ def tile_picked_skipflowbnorm_none_p_kernel(tc, x_words, x_scales, w1, gn, w2, o
                     first, final = (i == 0 and q == 0), (i == len(terms) - 1 and q == 3)
                     nc.tensor.matmul(target[:, cols], term[:, cols], identity[:], start=first, stop=final, is_transpose=True)
 
-        sum_turned = keep.tile([P, PACK, S], F32, tag="z_rows1")
+        sum_turned = keep.tile([P, PACK, S], F32, tag="recip")
         minus_sum = []
         for t in tiles:
             sum_bank = bank(4 + t, f"sum_bank{t}")
@@ -207,9 +229,13 @@ def tile_picked_skipflowbnorm_none_p_kernel(tc, x_words, x_scales, w1, gn, w2, o
             else:
                 partial = keep.tile([P, S], F32)
                 nc.vector.tensor_tensor(own[:], h[t], minus_sum[t][:], MULT)
-                nc.vector.tensor_tensor(far[:, halves[0]], h_window[t][:].indirect(n3_sb[:, list_halves[0]]), y_far[t][:, halves[0]], MULT)
-                nc.vector.tensor_tensor(partial[:], own[:], near[:], ADD)
-                nc.vector.tensor_tensor(far[:, halves[1]], h_window[t][:].indirect(n3_sb[:, list_halves[1]]), y_far[t][:, halves[1]], MULT)
-                for c in range(2):
-                    nc.vector.tensor_tensor(result[:, halves[c]], partial[:, halves[c]], far[:, halves[c]], ADD)
-                    nc.sync.dma_start(out_rows[t][:, :, halves[c]], result[:, halves[c]])
+                for first, width in TAIL:
+                    cols = slice(first, first + width)
+                    entries = n3_sb[:, first // 16 : (first + width) // 16]
+                    nc.vector.tensor_tensor(far[:, cols], h_window[t][:].indirect(entries), y_far[t][:, cols], MULT)
+                    if first == 0:
+                        nc.vector.tensor_tensor(partial[:], own[:], near[:], ADD)
+                for first, width in TAIL:
+                    cols = slice(first, first + width)
+                    nc.vector.tensor_tensor(result[:, cols], partial[:, cols], far[:, cols], ADD)
+                    nc.sync.dma_start(out_rows[t][:, :, cols], result[:, cols])

from contextlib import ExitStack

import concourse.mybir as mybir
from concourse.masks import make_identity

K, T, S, N, H = 512, 2048, 512, 512, 512
FLOPS = 2 * K * H * S + 2 * H * N * S

F32 = mybir.dt.float32
BF16 = mybir.dt.bfloat16
I32 = mybir.dt.int32
U32 = mybir.dt.uint32
U16 = mybir.dt.uint16
U8 = mybir.dt.uint8
FP8X4 = mybir.dt.float8_e4m3fn_x4
ACT = mybir.ActivationFunctionType
MULT = mybir.AluOpType.mult
MAX = mybir.AluOpType.max
ADD = mybir.AluOpType.add
SUBTRACT = mybir.AluOpType.subtract

P = 128
PACK = 4
HALF = S // 2
PIECES = [(0, 256, (0, 1)), (256, 128, (2,)), (384, 128, (3,))]
LIST_COLS = S // 16
TAIL = [(0, 384), (384, 128)]


def deal_weight(nc, raw, grouped):
    nc.vector.tensor_copy(
        out=grouped[:].rearrange("p (t a r j) -> p t a j r", t=PACK, r=4, j=PACK),
        in_=raw[:].rearrange("p j (a t r) -> p t a j r", t=PACK, r=4),
    )


def tile_picked_skipflowbnorm_none_p_kernel(tc, x_words, x_scales, w1, gn, w2, offs, n1, n2, n3, n4, out):
    nc = tc.nc
    tiles = range(PACK)
    halves = [slice(0, HALF), slice(HALF, S)]
    list_halves = [slice(0, LIST_COLS // 2), slice(LIST_COLS // 2, LIST_COLS)]
    out_rows = out.rearrange("(a t r) n -> t a r n", t=PACK, r=4)
    w2_rows = w2.rearrange("(a t r) n -> t a r n", t=PACK, r=4)
    gn_rows = gn.rearrange("(a t r) o -> t a r o", t=PACK, r=4)

    with ExitStack() as ctx:
        keep = ctx.enter_context(tc.tile_pool(name="keep", bufs=1))
        psum = ctx.enter_context(tc.psum_pool(name="psum", bufs=1))

        def bank(b, name):
            return psum.tile([P, S], F32, name=name, tag=f"bank{b}")

        def load_list(src, name):
            lst = keep.tile([P, LIST_COLS], U16, name=name)
            nc.sync.dma_start(lst[:], src)
            return lst

        x_bytes = keep.tile([P, T], U8, align_bytes=64)
        nc.gpsimd.memset(x_bytes[:].bitcast(I32), 0)
        offs_sb = load_list(offs, "offs_sb")
        for q in range(4):
            nc.sync.dma_start(x_bytes[32 * q : 32 * q + 4, :].bitcast(I32), x_scales[0, 4 * q : 4 * q + 4, :].bitcast(I32))
        w1_raw = keep.tile([P, PACK, H], F32)
        nc.sync.dma_start(w1_raw[:], w1.rearrange("(p j) c -> p j c", j=PACK))
        x_packed = keep.tile([P, T], I32, align_bytes=64)
        nc.sync.dma_start(x_packed[:], x_words[0].rearrange("p n t -> p (n t)").bitcast(I32))
        n1_sb = load_list(n1, "n1_sb")
        w2_raw = keep.tile([P, PACK, N], F32)
        for t in tiles:
            nc.sync.dma_start(w2_raw[:, t, :], w2_rows[t])
        n4_sb = load_list(n4, "n4_sb")
        gain = [keep.tile([P, 1], F32, name=f"gain{t}") for t in tiles]
        for t in tiles:
            nc.sync.dma_start(gain[t][:], gn_rows[t])
        n2_sb = load_list(n2, "n2_sb")
        n3_sb = load_list(n3, "n3_sb")

        half_const = keep.tile([P, 1], F32)
        nc.gpsimd.memset(half_const[:], 0.5)
        warm = keep.tile([P, 1], F32)
        nc.scalar.activation(warm[:], half_const[:], ACT.Ln)
        last = PACK - 1
        y_window = [keep.tile([P, 2 * S], F32, name=f"y_window{t}") for t in tiles]
        h_window = [keep.tile([P, 2 * S], F32, name=f"h_window{t}") for t in tiles]
        for t in tiles:
            nc.vector.memset(y_window[t][:, S : 2 * S], 0.0)
            nc.gpsimd.memset(h_window[t][:, S : 2 * S], 0.0)
        identity = keep.tile([P, P], F32)
        make_identity(nc, identity[:])

        picked_bytes = keep.tile([P, S], U8, align_bytes=64)
        nc.vector.tensor_copy(picked_bytes[:], x_bytes[:].indirect(offs_sb[:]))
        w1_codes, w1_scales = [], []
        w1_dealt = w1_raw[:].rearrange("p j (a t r) -> p t a j r", t=PACK, r=4)
        for pair, copy in enumerate((nc.vector.tensor_copy, nc.scalar.copy)):
            grouped = keep.tile([P, 2 * PACK * P], BF16, name=f"w1_grouped{pair}", align_bytes=64)
            copy(grouped[:].rearrange("p (t a r j) -> p t a j r", t=2, r=4, j=PACK), w1_dealt[:, 2 * pair : 2 * pair + 2])
            w1_codes.append(keep.tile([P, 2 * P], U32, name=f"w1_codes{pair}", align_bytes=64))
            w1_scales.append(keep.tile([P, 2 * P], U8, name=f"w1_scales{pair}", align_bytes=64))
            nc.vector.quantize_mx(out=w1_codes[pair][:].bitcast(FP8X4), scales=w1_scales[pair][:], in_=grouped[:])

        picked_words = []
        for c in range(2):
            picked_words.append(keep.tile([P, HALF], U32, name=f"picked_words{c}", align_bytes=64))
            nc.vector.tensor_copy(picked_words[c][:], x_packed[:].bitcast(U32).indirect(offs_sb[:, list_halves[c]]))

        log_window = [keep.tile([P, S], F32, name=f"log_window{t}") for t in tiles]
        y = [y_window[t][:, 0:S] for t in tiles]
        h = [h_window[t][:, 0:S] for t in tiles]
        y_abs = keep.tile([P, PACK, S], F32, tag="recip")
        for pair in range(2):
            pair_tiles = (2 * pair, 2 * pair + 1)
            for c in range(2):
                y_bank = bank(2 * pair + c, f"y_bank{pair}{c}")
                for u in range(2):
                    cols = slice(P * u, P * (u + 1))
                    nc.tensor.matmul_mx(
                        out=y_bank[:, halves[u]],
                        lhsT=w1_codes[pair][:, cols].bitcast(FP8X4),
                        lhsT_scale=w1_scales[pair][:, cols],
                        rhs=picked_words[c][:].bitcast(FP8X4),
                        rhs_scale=picked_bytes[:, halves[c]],
                        start=True,
                        stop=True,
                    )
                abs_on_vector = (pair, c) == (1, 0)
                if not abs_on_vector:
                    nc.scalar.activation(y_abs[:, 2 * pair : 2 * pair + 2, halves[c]], y_bank[:].rearrange("p (u n) -> p u n", u=2), ACT.Abs)
                for u, t in enumerate(pair_tiles):
                    nc.vector.tensor_copy(y[t][:, halves[c]], y_bank[:, halves[u]])
                if abs_on_vector:
                    for u, t in enumerate(pair_tiles):
                        nc.vector.scalar_tensor_tensor(y_abs[:, t, halves[c]], y_bank[:, halves[u]], -1.0, y[t][:, halves[c]], MULT, MAX)
            for t in pair_tiles:
                nc.scalar.activation(log_window[t][:], y_abs[:, t, :], ACT.Ln, bias=half_const[:])

        w2_grouped = keep.tile([P, PACK * N], BF16, align_bytes=64)
        w2_dealt = w2_raw[:].rearrange("p j (a t r) -> p t a r j", t=PACK, r=4)
        for t in tiles:
            target = w2_grouped[:, PACK * P * t : PACK * P * (t + 1)].rearrange("p (a r j) -> p a r j", r=4, j=PACK)
            nc.gpsimd.tensor_scalar(target, w2_dealt[:, t], 1.0, 0.0, MULT, ADD)
        w2_codes = keep.tile([P, N], U32, align_bytes=64)
        w2_scales = keep.tile([P, N], U8, align_bytes=64)
        nc.vector.quantize_mx(out=w2_codes[:].bitcast(FP8X4), scales=w2_scales[:], in_=w2_grouped[:])

        y_gain = keep.tile([P, PACK, S], F32)
        for t in tiles:
            nc.gpsimd.tensor_scalar(y_gain[:, t, :], y[t], gain[t][:], 0.0, MULT, ADD)

        pieces = PIECES
        recip = keep.tile([P, PACK, S], F32, tag="recip")
        recip_last = keep.tile([P, S], F32)
        nc.scalar.activation(recip_last[:], log_window[last][:], ACT.Exp, scale=-1.0)
        for c in range(2):
            nc.vector.tensor_copy(recip[:, last, halves[c]], recip_last[:].indirect(n1_sb[:, list_halves[c]]))
        for first, width, banks in pieces:
            for t in range(last):
                entries = n1_sb[:, first // 16 : (first + width) // 16]
                nc.scalar.activation(recip[:, t, first : first + width], log_window[t][:].indirect(entries), ACT.Exp, scale=-1.0)

        for g, (first, width, banks) in enumerate(pieces):
            z_grouped = keep.tile([P, PACK * width], BF16, name=f"z_grouped{g}", tag=f"z_grouped{g}", align_bytes=64)
            nc.vector.tensor_tensor(
                z_grouped[:].rearrange("p (c i t) -> p c t i", i=4, t=PACK),
                y_gain[:, :, first : first + width].rearrange("p t (c i) -> p c t i", i=4),
                recip[:, :, first : first + width].rearrange("p t (c i) -> p c t i", i=4),
                MULT,
            )
            z_codes = keep.tile([P, width], U32, name=f"z_codes{g}", align_bytes=64)
            z_scales = keep.tile([P, width], U8, name=f"z_scales{g}", align_bytes=64)
            nc.vector.quantize_mx(out=z_codes[:].bitcast(FP8X4), scales=z_scales[:], in_=z_grouped[:])
            per_bank = S // width
            for b, number in enumerate(banks):
                h_bank = bank(number, f"h_bank{g}{b}")
                for u in range(per_bank):
                    t = per_bank * b + u
                    cols = slice(P * t, P * (t + 1))
                    nc.tensor.matmul_mx(
                        out=h_bank[:, width * u : width * (u + 1)],
                        lhsT=w2_codes[:, cols].bitcast(FP8X4),
                        lhsT_scale=w2_scales[:, cols],
                        rhs=z_codes[:].bitcast(FP8X4),
                        rhs_scale=z_scales[:],
                        start=True,
                        stop=True,
                    )
                for u in range(per_bank):
                    t = per_bank * b + u
                    nc.scalar.copy(h[t][:, first : first + width], h_bank[:, width * u : width * (u + 1)])

        y_far = [keep.tile([P, S], F32, name=f"y_far{t}") for t in range(last)]
        y_far.append(keep.tile([P, S], F32, name="y_far_last", tag=f"z_grouped{len(pieces) - 1}", align_bytes=64))
        for t in tiles:
            nc.vector.tensor_scalar(y_far[t][:], y_window[t][:].indirect(n4_sb[:]), 0.5, 0.0, MULT, ADD)

        def add_turned(target, terms):
            for i, term in enumerate(terms):
                for q in range(4):
                    cols = slice(P * q, P * (q + 1))
                    first, final = (i == 0 and q == 0), (i == len(terms) - 1 and q == 3)
                    nc.tensor.matmul(target[:, cols], term[:, cols], identity[:], start=first, stop=final, is_transpose=True)

        sum_turned = keep.tile([P, PACK, S], F32, tag="recip")
        minus_sum = []
        for t in tiles:
            sum_bank = bank(4 + t, f"sum_bank{t}")
            add_turned(sum_bank, (y[t], y_far[t]))
            nc.scalar.activation(sum_turned[:, t, :], sum_bank[:], ACT.Copy, scale=-1.0)
            minus_sum.append(bank(4 + t, f"minus_sum{t}"))
            add_turned(minus_sum[t], (sum_turned[:, t, :],))

        for t in tiles:
            near = keep.tile([P, S], F32, name=f"near{t}")
            far = keep.tile([P, S], F32, name=f"far{t}")
            own = keep.tile([P, S], F32, name=f"own{t}")
            result = keep.tile([P, S], F32, name=f"result{t}")
            nc.vector.tensor_tensor(near[:], h_window[t][:].indirect(n2_sb[:]), y[t], MULT)
            if t < last:
                nc.vector.tensor_tensor(far[:], h_window[t][:].indirect(n3_sb[:]), y_far[t][:], MULT)
                nc.vector.tensor_tensor(own[:], h[t], minus_sum[t][:], MULT)
                turned_bank = bank(t % 2, f"turned_bank{t}")
                add_turned(turned_bank, (near, far, own))
                turned = keep.tile([P, S], F32, name=f"turned{t}")
                nc.scalar.copy(turned[:], turned_bank[:])
                back_bank = bank(2 + t % 2, f"back_bank{t}")
                add_turned(back_bank, (turned,))
                nc.scalar.copy(result[:], back_bank[:])
                nc.sync.dma_start(out_rows[t], result[:])
            else:
                partial = keep.tile([P, S], F32)
                nc.vector.tensor_tensor(own[:], h[t], minus_sum[t][:], MULT)
                for first, width in TAIL:
                    cols = slice(first, first + width)
                    entries = n3_sb[:, first // 16 : (first + width) // 16]
                    nc.vector.tensor_tensor(far[:, cols], h_window[t][:].indirect(entries), y_far[t][:, cols], MULT)
                    if first == 0:
                        nc.vector.tensor_tensor(partial[:], own[:], near[:], ADD)
                for first, width in TAIL:
                    cols = slice(first, first + width)
                    nc.vector.tensor_tensor(result[:, cols], partial[:, cols], far[:, cols], ADD)
                    nc.sync.dma_start(out_rows[t][:, :, cols], result[:, cols])
